import numpy as np, ml_dtypes
CORES = [6,14,30,38,62,70,86,94,102]
N = 9
F = 512
def setup_inputs(rng):
    return {"a": rng.standard_normal((N, 128, 128), dtype=np.float32).astype(ml_dtypes.bfloat16), "w": rng.standard_normal((N, 128, F), dtype=np.float32).astype(ml_dtypes.bfloat16)}
def setup_inputs_big(rng):
    d = setup_inputs(rng)
    for k in ("a", "w"): d[k] = (d[k].astype(np.float32) * 1024.0).astype(d[k].dtype)
    return d
def setup_inputs_small(rng):
    d = setup_inputs(rng)
    for k in ("a", "w"): d[k] = (d[k].astype(np.float32) * (1 / 1024.0)).astype(d[k].dtype)
    return d
def setup_inputs_apart(rng):
    d = setup_inputs(rng)
    f = (10.0 ** rng.permutation(np.linspace(-1.5, 1.5, N))).astype(np.float32).reshape(N, 1, 1)
    for k in ("a", "w"): d[k] = (d[k].astype(np.float32) * f).astype(d[k].dtype)
    return d
def reference(a, w):
    A, W = a.astype(np.float64), w.astype(np.float64)
    p = np.stack([A[j].T @ W[j] for j in range(N)])
    return {"y": np.cumsum(p, axis=0).astype(ml_dtypes.bfloat16 if a.dtype != np.float64 else np.float64)}

@@ -1,0 +1,129 @@
+from concourse.bass import DstId, RemoteDMATransfer
+from concourse.mybir import AluOpType
+
+GROUP = 3
+F = 512
+
+SCRATCH = {
+    "asb": ("sbuf", [128, 128], "bfloat16"),
+    "wsb": ("sbuf", [128, F], "bfloat16"),
+    "ps": ("psum", [128, F], "float32"),
+    "pb": ("sbuf", [128, F], "bfloat16"),
+    "yb": ("sbuf", [128, F], "bfloat16"),
+    "raw0": ("sbuf", [128, F], "bfloat16"),
+    "raw1": ("sbuf", [128, F], "bfloat16"),
+    "raw2": ("sbuf", [128, F], "bfloat16"),
+    "sum0": ("sbuf", [128, F], "bfloat16"),
+    "sum1": ("sbuf", [128, F], "bfloat16"),
+}
+SEMAPHORES = ["ld", "mm", "vs", "raw0", "raw1", "raw2", "sum0", "sum1", "sent", "st"]
+
+
+def _hops(topo, s, d):
+    a, b = topo.chip(s), topo.chip(d)
+    if a == b:
+        return 0
+    return 1 if (topo.mates(a, b) or topo.same_plane(a, b)) else 2
+
+
+def _plan(cores, topo):
+    n = len(cores)
+    groups = [list(range(k, min(k + GROUP, n))) for k in range(0, n, GROUP)]
+    raw_to = {r: [] for r in range(n)}
+    sum_to = {r: [] for r in range(n)}
+    for m in groups:
+        later = list(range(m[-1] + 1, n))
+        for r in m:
+            raw_to[r] = [q for q in m if q != r and (q > r or later)]
+        if not later:
+            continue
+        cap = -(-len(later) // len(m))
+        pairs = sorted((_hops(topo, cores[s], cores[d]), s, d)
+                       for s in m for d in later if topo.may_write(cores[s], cores[d]))
+        done = set()
+        for _, s, d in pairs:
+            if d not in done and len(sum_to[s]) < cap:
+                sum_to[s].append(d)
+                done.add(d)
+        assert len(done) == len(later)
+    return groups, raw_to, sum_to
+
+
+def _mask(topo, src, dsts):
+    m = topo.mask(src, dsts[0])
+    for d in dsts[1:]:
+        m &= topo.mask(src, d)
+    return m
+
+
+def _count(mask):
+    return bin(mask).count("1")
+
+
+def rank_program(g, core, T, topo):
+    rank = T.rank_of(core)
+    if rank is None:
+        return
+    cores = list(T.cores)
+    groups, raw_to, sum_to = _plan(cores, topo)
+    gi = rank // GROUP
+    members = groups[gi]
+    me = rank - members[0]
+
+    def width(sender, table):
+        return _count(_mask(topo, cores[sender], [cores[d] for d in table[sender]]))
+
+    def send(srcs, buf, sem, dst_ranks):
+        dst = [cores[d] for d in dst_ranks]
+        for d in dst:
+            assert topo.may_write(core, d)
+        mask = _mask(topo, core, dst)
+        ids = []
+        for d in dst:
+            rid, pid, _ = topo.addr(d)
+            ids.append(DstId(rid=rid, pnc=pid))
+        g.remote_dma_fused(
+            [RemoteDMATransfer(dst_ids=ids, dma_engine_mask=mask, remote_sem=sem, srcs=srcs,
+                               dsts=[buf[:] for _ in dst], alu_op=(1 if len(srcs) > 1 else 0))],
+            local_sem=T.sem.sent)
+        return _count(mask)
+
+    g.sync.dma_start(T.asb[:], T.a[:]).then_inc(T.sem.ld, 16)
+    g.scalar.dma_start(T.wsb[:], T.w[:]).then_inc(T.sem.ld, 16)
+    g.tensor.wait_ge(T.sem.ld, 32)
+    g.tensor.matmul(T.ps[:], T.asb[:], T.wsb[:], True, True).then_inc(T.sem.mm, 1)
+
+    g.vector.wait_ge(T.sem.mm, 1)
+    nv = 0
+    terms = [("raw%d" % k, width(members[k], raw_to)) for k in range(me)]
+    for q in range(gi - 1, -1, -1):
+        s = [x for x in groups[q] if rank in sum_to[x]][0]
+        terms.append(("sum%d" % q, width(s, sum_to)))
+    if raw_to[rank] or not terms:
+        g.vector.tensor_copy(T.pb[:], T.ps[:]).then_inc(T.sem.vs, 1)
+        nv = 1
+    for k, (name, w) in enumerate(terms):
+        g.vector.wait_ge(T.sem[name], w)
+        if nv:
+            g.vector.wait_ge(T.sem.vs, nv)
+        out = T.yb if k == len(terms) - 1 else T.ps
+        g.vector.tensor_tensor(out[:], T.ps[:], T[name][:], AluOpType.add).then_inc(T.sem.vs, 1)
+        nv += 1
+
+    sent = 0
+    if raw_to[rank]:
+        g.wait_ge(T.sem.vs, 1)
+        sent += send([T.pb[:]], T["raw%d" % me], T.sem["raw%d" % me], raw_to[rank])
+    if sum_to[rank]:
+        srcs = [T.pb[:]]
+        for k, q in enumerate(members):
+            if q != rank:
+                g.wait_ge(T.sem["raw%d" % k], width(q, raw_to))
+                srcs.append(T["raw%d" % k][:])
+        sent += send(srcs, T["sum%d" % gi], T.sem["sum%d" % gi], sum_to[rank])
+
+    g.sync.wait_ge(T.sem.vs, nv)
+    g.sync.dma_start(T.y[:], (T.yb if terms else T.pb)[:]).then_inc(T.sem.st, 16)
+    g.sync.wait_ge(T.sem.st, 16)
+    if sent:
+        g.wait_ge(T.sem.sent, sent)

@@ -2,21 +2,25 @@ from concourse.bass import DstId, RemoteDMATransfer
 from concourse.mybir import AluOpType
 
 GROUP = 3
+K = 128
 F = 512
 
 SCRATCH = {
-    "asb": ("sbuf", [128, 128], "bfloat16"),
-    "wsb": ("sbuf", [128, F], "bfloat16"),
+    "xb": ("sbuf", [128, K + F], "bfloat16"),
+    "xr": ("sbuf", [128, K + F], "bfloat16"),
     "ps": ("psum", [128, F], "float32"),
+    "pg": ("psum", [128, F], "float32"),
     "pb": ("sbuf", [128, F], "bfloat16"),
+    "gs": ("sbuf", [128, F], "bfloat16"),
     "yb": ("sbuf", [128, F], "bfloat16"),
-    "raw0": ("sbuf", [128, F], "bfloat16"),
-    "raw1": ("sbuf", [128, F], "bfloat16"),
-    "raw2": ("sbuf", [128, F], "bfloat16"),
-    "sum0": ("sbuf", [128, F], "bfloat16"),
-    "sum1": ("sbuf", [128, F], "bfloat16"),
 }
-SEMAPHORES = ["ld", "mm", "vs", "raw0", "raw1", "raw2", "sum0", "sum1", "sent", "st"]
+SEMAPHORES = ["ld", "mm", "mg", "vs", "xs", "sent", "st"]
+for _k in range(GROUP):
+    SCRATCH["raw%d" % _k] = ("sbuf", [128, F], "bfloat16")
+    SEMAPHORES.append("raw%d" % _k)
+for _k in range(2):
+    SCRATCH["sum%d" % _k] = ("sbuf", [128, F], "bfloat16")
+    SEMAPHORES.append("sum%d" % _k)
 
 
 def _hops(topo, s, d):
@@ -29,12 +33,9 @@ def _hops(topo, s, d):
 def _plan(cores, topo):
     n = len(cores)
     groups = [list(range(k, min(k + GROUP, n))) for k in range(0, n, GROUP)]
-    raw_to = {r: [] for r in range(n)}
     sum_to = {r: [] for r in range(n)}
     for m in groups:
         later = list(range(m[-1] + 1, n))
-        for r in m:
-            raw_to[r] = [q for q in m if q != r and (q > r or later)]
         if not later:
             continue
         cap = -(-len(later) // len(m))
@@ -46,7 +47,7 @@ def _plan(cores, topo):
                 sum_to[s].append(d)
                 done.add(d)
         assert len(done) == len(later)
-    return groups, raw_to, sum_to
+    return groups, sum_to
 
 
 def _mask(topo, src, dsts):
@@ -65,15 +66,19 @@ def rank_program(g, core, T, topo):
     if rank is None:
         return
     cores = list(T.cores)
-    groups, raw_to, sum_to = _plan(cores, topo)
+    groups, sum_to = _plan(cores, topo)
     gi = rank // GROUP
     members = groups[gi]
     me = rank - members[0]
+    add = AluOpType.add
+    ring = bool(sum_to[rank])
+    assert not ring or len(members) == 3
+    a_own, w_own = T.xb[:, 0:K], T.xb[:, K:K + F]
 
-    def width(sender, table):
-        return _count(_mask(topo, cores[sender], [cores[d] for d in table[sender]]))
+    def width(sender, dst_ranks):
+        return _count(_mask(topo, cores[sender], [cores[d] for d in dst_ranks]))
 
-    def send(srcs, buf, sem, dst_ranks):
+    def send(src, buf, sem, dst_ranks):
         dst = [cores[d] for d in dst_ranks]
         for d in dst:
             assert topo.may_write(core, d)
@@ -83,47 +88,83 @@ def rank_program(g, core, T, topo):
             rid, pid, _ = topo.addr(d)
             ids.append(DstId(rid=rid, pnc=pid))
         g.remote_dma_fused(
-            [RemoteDMATransfer(dst_ids=ids, dma_engine_mask=mask, remote_sem=sem, srcs=srcs,
-                               dsts=[buf[:] for _ in dst], alu_op=(1 if len(srcs) > 1 else 0))],
+            [RemoteDMATransfer(dst_ids=ids, dma_engine_mask=mask, remote_sem=sem, srcs=[src[:]],
+                               dsts=[buf[:] for _ in dst], alu_op=0)],
             local_sem=T.sem.sent)
         return _count(mask)
 
-    g.sync.dma_start(T.asb[:], T.a[:]).then_inc(T.sem.ld, 16)
-    g.scalar.dma_start(T.wsb[:], T.w[:]).then_inc(T.sem.ld, 16)
+    g.sync.dma_start(a_own, T.a[:]).then_inc(T.sem.ld, 16)
+    g.scalar.dma_start(w_own, T.w[:]).then_inc(T.sem.ld, 16)
     g.tensor.wait_ge(T.sem.ld, 32)
-    g.tensor.matmul(T.ps[:], T.asb[:], T.wsb[:], True, True).then_inc(T.sem.mm, 1)
+    g.tensor.matmul(T.ps[:], a_own, w_own, True, True).then_inc(T.sem.mm, 1)
 
-    g.vector.wait_ge(T.sem.mm, 1)
-    nv = 0
-    terms = [("raw%d" % k, width(members[k], raw_to)) for k in range(me)]
+    sums = []
     for q in range(gi - 1, -1, -1):
         s = [x for x in groups[q] if rank in sum_to[x]][0]
-        terms.append(("sum%d" % q, width(s, sum_to)))
-    if raw_to[rank] or not terms:
-        g.vector.tensor_copy(T.pb[:], T.ps[:]).then_inc(T.sem.vs, 1)
-        nv = 1
-    for k, (name, w) in enumerate(terms):
+        sums.append(("sum%d" % q, width(s, sum_to[s])))
+
+    nv = [0]
+
+    def vec(out, in0, name, w):
         g.vector.wait_ge(T.sem[name], w)
-        if nv:
-            g.vector.wait_ge(T.sem.vs, nv)
-        out = T.yb if k == len(terms) - 1 else T.ps
-        g.vector.tensor_tensor(out[:], T.ps[:], T[name][:], AluOpType.add).then_inc(T.sem.vs, 1)
-        nv += 1
+        if nv[0]:
+            g.vector.wait_ge(T.sem.vs, nv[0])
+        g.vector.tensor_tensor(out[:], in0[:], T[name][:], add).then_inc(T.sem.vs, 1)
+        nv[0] += 1
 
     sent = 0
-    if raw_to[rank]:
+    if ring:
+        nxt, prv = (me + 1) % 3, (me + 2) % 3
+        g.tensor.matmul(T.pg[:], a_own, w_own, True, False)
+        g.tensor.wait_ge(T.sem.xs, width(members[prv], [rank]))
+        g.tensor.matmul(T.pg[:], T.xr[:, 0:K], T.xr[:, K:K + F], False, True).then_inc(T.sem.mg, 1)
+        g.vector.wait_ge(T.sem.mm, 1)
+        g.vector.tensor_copy(T.pb[:], T.ps[:]).then_inc(T.sem.vs, 1)
+        nv[0] = 1
+        g.vector.wait_ge(T.sem.mg, 1)
+        late = ("raw%d" % nxt, width(members[nxt], [rank]))
+        vec(T.gs, T.pg, late[0], late[1])
+        gat = nv[0]
+        own_only = prv > me
+        acc = T.ps if own_only else T.pg
+        yterms = ([late] if nxt < me else []) + sums
+        if yterms == [late]:
+            ysrc, yat = T.gs, gat
+        elif not yterms and own_only:
+            ysrc, yat = T.pb, 1
+        elif not yterms:
+            g.vector.wait_ge(T.sem.vs, nv[0])
+            g.vector.tensor_copy(T.yb[:], acc[:]).then_inc(T.sem.vs, 1)
+            nv[0] += 1
+            ysrc, yat = T.yb, nv[0]
+        else:
+            for n, (name, w) in enumerate(yterms):
+                vec(T.yb if n == len(yterms) - 1 else acc, acc, name, w)
+            ysrc, yat = T.yb, nv[0]
+        g.wait_ge(T.sem.ld, 32)
+        sent += send(T.xb, T.xr, T.sem.xs, [members[nxt]])
         g.wait_ge(T.sem.vs, 1)
-        sent += send([T.pb[:]], T["raw%d" % me], T.sem["raw%d" % me], raw_to[rank])
-    if sum_to[rank]:
-        srcs = [T.pb[:]]
-        for k, q in enumerate(members):
-            if q != rank:
-                g.wait_ge(T.sem["raw%d" % k], width(q, raw_to))
-                srcs.append(T["raw%d" % k][:])
-        sent += send(srcs, T["sum%d" % gi], T.sem["sum%d" % gi], sum_to[rank])
+        sent += send(T.pb, T["raw%d" % me], T.sem["raw%d" % me], [members[prv]])
+        g.wait_ge(T.sem.vs, gat)
+        sent += send(T.gs, T["sum%d" % gi], T.sem["sum%d" % gi], sum_to[rank])
+    else:
+        after = members[me + 1:]
+        g.vector.wait_ge(T.sem.mm, 1)
+        if after:
+            g.vector.tensor_copy(T.pb[:], T.ps[:]).then_inc(T.sem.vs, 1)
+            nv[0] = 1
+        yterms = [("raw%d" % k, width(members[k], members[k + 1:])) for k in range(me - 1, -1, -1)] + sums
+        assert yterms
+        for n, (name, w) in enumerate(yterms):
+            vec(T.yb if n == len(yterms) - 1 else T.ps, T.ps, name, w)
+        ysrc, yat = T.yb, nv[0]
+        if after:
+            g.wait_ge(T.sem.vs, 1)
+            sent += send(T.pb, T["raw%d" % me], T.sem["raw%d" % me], after)
 
-    g.sync.wait_ge(T.sem.vs, nv)
-    g.sync.dma_start(T.y[:], (T.yb if terms else T.pb)[:]).then_inc(T.sem.st, 16)
+    g.sync.wait_ge(T.sem.vs, yat)
+    g.sync.dma_start(T.y[:], ysrc[:]).then_inc(T.sem.st, 16)
     g.sync.wait_ge(T.sem.st, 16)
+    g.wait_ge(T.sem.vs, nv[0])
     if sent:
         g.wait_ge(T.sem.sent, sent)

@@ -4,17 +4,22 @@ from concourse.mybir import AluOpType
 GROUP = 3
 K = 128
 F = 512
+H = F // 2
 
 SCRATCH = {
-    "xb": ("sbuf", [128, K + F], "bfloat16"),
-    "xr": ("sbuf", [128, K + F], "bfloat16"),
+    "xa": ("sbuf", [128, K], "bfloat16"),
+    "xw": ("sbuf", [128, F], "bfloat16"),
+    "ad": ("dram", [128, K], "bfloat16"),
+    "ar": ("dram", [128, K], "bfloat16"),
+    "ra": ("sbuf", [128, K], "bfloat16"),
+    "rw": ("sbuf", [128, F], "bfloat16"),
     "ps": ("psum", [128, F], "float32"),
     "pg": ("psum", [128, F], "float32"),
     "pb": ("sbuf", [128, F], "bfloat16"),
     "gs": ("sbuf", [128, F], "bfloat16"),
     "yb": ("sbuf", [128, F], "bfloat16"),
 }
-SEMAPHORES = ["ld", "mm", "mg", "vs", "xs", "sent", "st"]
+SEMAPHORES = ["lc", "la", "lw", "lr", "ax", "xs", "mm", "mg", "vs", "sent", "st"]
 for _k in range(GROUP):
     SCRATCH["raw%d" % _k] = ("sbuf", [128, F], "bfloat16")
     SEMAPHORES.append("raw%d" % _k)
@@ -50,6 +55,18 @@ def _plan(cores, topo):
     return groups, sum_to
 
 
+def _turn(cores, topo, members, sum_to):
+    best = None
+    for d in (1, -1):
+        worst = 0
+        for i, r in enumerate(members):
+            src = members[(i + d) % len(members)]
+            worst = max(worst, _hops(topo, cores[src], cores[r]) + max(_hops(topo, cores[r], cores[x]) for x in sum_to[r]))
+        if best is None or worst < best[0]:
+            best = (worst, d)
+    return best[1]
+
+
 def _mask(topo, src, dsts):
     m = topo.mask(src, dsts[0])
     for d in dsts[1:]:
@@ -59,6 +76,16 @@ def _mask(topo, src, dsts):
 
 def _count(mask):
     return bin(mask).count("1")
+
+
+def _transfers(topo, src, dsts):
+    m = _mask(topo, src, dsts)
+    e = [b for b in range(m.bit_length()) if (m >> b) & 1]
+    n = len(dsts)
+    if n > 1 and len(e) % n == 0 and 128 % (len(e) // n) == 0:
+        k = len(e) // n
+        return [(sum(1 << b for b in e[i * k:(i + 1) * k]), [dsts[i]]) for i in range(n)]
+    return [(m, list(dsts))]
 
 
 def rank_program(g, core, T, topo):
@@ -73,35 +100,39 @@ def rank_program(g, core, T, topo):
     add = AluOpType.add
     ring = bool(sum_to[rank])
     assert not ring or len(members) == 3
-    a_own, w_own = T.xb[:, 0:K], T.xb[:, K:K + F]
 
-    def width(sender, dst_ranks):
-        return _count(_mask(topo, cores[sender], [cores[d] for d in dst_ranks]))
+    def width(sender, dst_ranks, to):
+        for mask, ds in _transfers(topo, cores[sender], [cores[d] for d in dst_ranks]):
+            if cores[to] in ds:
+                return _count(mask)
+        assert False
 
     def send(src, buf, sem, dst_ranks):
-        dst = [cores[d] for d in dst_ranks]
-        for d in dst:
-            assert topo.may_write(core, d)
-        mask = _mask(topo, core, dst)
-        ids = []
-        for d in dst:
-            rid, pid, _ = topo.addr(d)
-            ids.append(DstId(rid=rid, pnc=pid))
-        g.remote_dma_fused(
-            [RemoteDMATransfer(dst_ids=ids, dma_engine_mask=mask, remote_sem=sem, srcs=[src[:]],
-                               dsts=[buf[:] for _ in dst], alu_op=0)],
-            local_sem=T.sem.sent)
-        return _count(mask)
+        trs, tot = [], 0
+        for mask, ds in _transfers(topo, core, [cores[d] for d in dst_ranks]):
+            ids = []
+            for d in ds:
+                assert topo.may_write(core, d)
+                rid, pid, _ = topo.addr(d)
+                ids.append(DstId(rid=rid, pnc=pid))
+            trs.append(RemoteDMATransfer(dst_ids=ids, dma_engine_mask=mask, remote_sem=sem, srcs=[src[:]],
+                                         dsts=[buf[:] for _ in ds], alu_op=0))
+            tot += _count(mask)
+        g.remote_dma_fused(trs, local_sem=T.sem.sent)
+        return tot
 
-    g.sync.dma_start(a_own, T.a[:]).then_inc(T.sem.ld, 16)
-    g.scalar.dma_start(w_own, T.w[:]).then_inc(T.sem.ld, 16)
-    g.tensor.wait_ge(T.sem.ld, 32)
-    g.tensor.matmul(T.ps[:], a_own, w_own, True, True).then_inc(T.sem.mm, 1)
+    if ring:
+        g.sync.dma_start(T.ad[:], T.a[:]).then_inc(T.sem.lc, 16)
+    g.scalar.dma_start(T.xw[:], T.w[:]).then_inc(T.sem.lw, 16)
+    g.scalar.dma_start(T.xa[:], T.a[:]).then_inc(T.sem.la, 16)
+    g.tensor.wait_ge(T.sem.la, 16)
+    g.tensor.wait_ge(T.sem.lw, 16)
+    g.tensor.matmul(T.ps[:], T.xa[:], T.xw[:], True, True).then_inc(T.sem.mm, 1)
 
     sums = []
     for q in range(gi - 1, -1, -1):
         s = [x for x in groups[q] if rank in sum_to[x]][0]
-        sums.append(("sum%d" % q, width(s, sum_to[s])))
+        sums.append(("sum%d" % q, width(s, sum_to[s], rank)))
 
     nv = [0]
 
@@ -112,23 +143,39 @@ def rank_program(g, core, T, topo):
         g.vector.tensor_tensor(out[:], in0[:], T[name][:], add).then_inc(T.sem.vs, 1)
         nv[0] += 1
 
+    def finish(acc, yterms):
+        for name, w in yterms[:-1]:
+            vec(acc, acc, name, w)
+        name, w = yterms[-1]
+        g.vector.wait_ge(T.sem[name], w)
+        if nv[0]:
+            g.vector.wait_ge(T.sem.vs, nv[0])
+        for lo, hi in ((0, H), (H, F)):
+            g.vector.tensor_tensor(T.yb[:, lo:hi], acc[:, lo:hi], T[name][:, lo:hi], add).then_inc(T.sem.vs, 1)
+            nv[0] += 1
+
     sent = 0
+    halves = False
     if ring:
-        nxt, prv = (me + 1) % 3, (me + 2) % 3
-        g.tensor.matmul(T.pg[:], a_own, w_own, True, False)
-        g.tensor.wait_ge(T.sem.xs, width(members[prv], [rank]))
-        g.tensor.matmul(T.pg[:], T.xr[:, 0:K], T.xr[:, K:K + F], False, True).then_inc(T.sem.mg, 1)
+        d = _turn(cores, topo, members, sum_to)
+        nxt, prv = (me + d) % 3, (me - d) % 3
+        g.sync.wait_ge(T.sem.ax, width(members[prv], [rank], rank))
+        g.sync.dma_start(T.ra[:], T.ar[:]).then_inc(T.sem.lr, 16)
+        g.tensor.matmul(T.pg[:], T.xa[:], T.xw[:], True, False)
+        g.tensor.wait_ge(T.sem.lr, 16)
+        g.tensor.wait_ge(T.sem.xs, width(members[prv], [rank], rank))
+        g.tensor.matmul(T.pg[:], T.ra[:], T.rw[:], False, True).then_inc(T.sem.mg, 1)
         g.vector.wait_ge(T.sem.mm, 1)
         g.vector.tensor_copy(T.pb[:], T.ps[:]).then_inc(T.sem.vs, 1)
         nv[0] = 1
         g.vector.wait_ge(T.sem.mg, 1)
-        late = ("raw%d" % nxt, width(members[nxt], [rank]))
+        late = ("raw%d" % nxt, width(members[nxt], [rank], rank))
         vec(T.gs, T.pg, late[0], late[1])
         gat = nv[0]
         own_only = prv > me
         acc = T.ps if own_only else T.pg
         yterms = ([late] if nxt < me else []) + sums
-        if yterms == [late]:
+        if yterms == [late] and not own_only:
             ysrc, yat = T.gs, gat
         elif not yterms and own_only:
             ysrc, yat = T.pb, 1
@@ -138,11 +185,12 @@ def rank_program(g, core, T, topo):
             nv[0] += 1
             ysrc, yat = T.yb, nv[0]
         else:
-            for n, (name, w) in enumerate(yterms):
-                vec(T.yb if n == len(yterms) - 1 else acc, acc, name, w)
-            ysrc, yat = T.yb, nv[0]
-        g.wait_ge(T.sem.ld, 32)
-        sent += send(T.xb, T.xr, T.sem.xs, [members[nxt]])
+            finish(acc, yterms)
+            ysrc, yat, halves = T.yb, nv[0], True
+        g.wait_ge(T.sem.lc, 16)
+        sent += send(T.ad, T.ar, T.sem.ax, [members[nxt]])
+        g.wait_ge(T.sem.lw, 16)
+        sent += send(T.xw, T.rw, T.sem.xs, [members[nxt]])
         g.wait_ge(T.sem.vs, 1)
         sent += send(T.pb, T["raw%d" % me], T.sem["raw%d" % me], [members[prv]])
         g.wait_ge(T.sem.vs, gat)
@@ -153,18 +201,24 @@ def rank_program(g, core, T, topo):
         if after:
             g.vector.tensor_copy(T.pb[:], T.ps[:]).then_inc(T.sem.vs, 1)
             nv[0] = 1
-        yterms = [("raw%d" % k, width(members[k], members[k + 1:])) for k in range(me - 1, -1, -1)] + sums
+        yterms = [("raw%d" % k, width(members[k], members[k + 1:], rank)) for k in range(me - 1, -1, -1)] + sums
         assert yterms
-        for n, (name, w) in enumerate(yterms):
-            vec(T.yb if n == len(yterms) - 1 else T.ps, T.ps, name, w)
-        ysrc, yat = T.yb, nv[0]
+        finish(T.ps, yterms)
+        ysrc, yat, halves = T.yb, nv[0], True
         if after:
             g.wait_ge(T.sem.vs, 1)
             sent += send(T.pb, T["raw%d" % me], T.sem["raw%d" % me], after)
 
-    g.sync.wait_ge(T.sem.vs, yat)
-    g.sync.dma_start(T.y[:], ysrc[:]).then_inc(T.sem.st, 16)
-    g.sync.wait_ge(T.sem.st, 16)
+    if halves:
+        g.sync.wait_ge(T.sem.vs, yat - 1)
+        g.sync.dma_start(T.y[:, 0:H], ysrc[:, 0:H]).then_inc(T.sem.st, 16)
+        g.scalar.wait_ge(T.sem.vs, yat)
+        g.scalar.dma_start(T.y[:, H:F], ysrc[:, H:F]).then_inc(T.sem.st, 16)
+        g.sync.wait_ge(T.sem.st, 32)
+    else:
+        g.sync.wait_ge(T.sem.vs, yat)
+        g.sync.dma_start(T.y[:], ysrc[:]).then_inc(T.sem.st, 16)
+        g.sync.wait_ge(T.sem.st, 16)
     g.wait_ge(T.sem.vs, nv[0])
     if sent:
         g.wait_ge(T.sem.sent, sent)

from concourse.bass import DstId, RemoteDMATransfer
from concourse.mybir import AluOpType

GROUP = 3
K = 128
F = 512
H = F // 2

SCRATCH = {
    "xa": ("sbuf", [128, K], "bfloat16"),
    "xw": ("sbuf", [128, F], "bfloat16"),
    "ad": ("dram", [128, K], "bfloat16"),
    "ar": ("dram", [128, K], "bfloat16"),
    "ra": ("sbuf", [128, K], "bfloat16"),
    "rw": ("sbuf", [128, F], "bfloat16"),
    "ps": ("psum", [128, F], "float32"),
    "pg": ("psum", [128, F], "float32"),
    "pb": ("sbuf", [128, F], "bfloat16"),
    "gs": ("sbuf", [128, F], "bfloat16"),
    "yb": ("sbuf", [128, F], "bfloat16"),
}
SEMAPHORES = ["lc", "la", "lw", "lr", "ax", "xs", "mm", "mg", "vs", "sent", "st"]
for _k in range(GROUP):
    SCRATCH["raw%d" % _k] = ("sbuf", [128, F], "bfloat16")
    SEMAPHORES.append("raw%d" % _k)
for _k in range(2):
    SCRATCH["sum%d" % _k] = ("sbuf", [128, F], "bfloat16")
    SEMAPHORES.append("sum%d" % _k)


def _hops(topo, s, d):
    a, b = topo.chip(s), topo.chip(d)
    if a == b:
        return 0
    return 1 if (topo.mates(a, b) or topo.same_plane(a, b)) else 2


def _plan(cores, topo):
    n = len(cores)
    groups = [list(range(k, min(k + GROUP, n))) for k in range(0, n, GROUP)]
    sum_to = {r: [] for r in range(n)}
    for m in groups:
        later = list(range(m[-1] + 1, n))
        if not later:
            continue
        cap = -(-len(later) // len(m))
        pairs = sorted((_hops(topo, cores[s], cores[d]), s, d)
                       for s in m for d in later if topo.may_write(cores[s], cores[d]))
        done = set()
        for _, s, d in pairs:
            if d not in done and len(sum_to[s]) < cap:
                sum_to[s].append(d)
                done.add(d)
        assert len(done) == len(later)
    return groups, sum_to


def _turn(cores, topo, members, sum_to):
    best = None
    for d in (1, -1):
        worst = 0
        for i, r in enumerate(members):
            src = members[(i + d) % len(members)]
            worst = max(worst, _hops(topo, cores[src], cores[r]) + max(_hops(topo, cores[r], cores[x]) for x in sum_to[r]))
        if best is None or worst < best[0]:
            best = (worst, d)
    return best[1]


def _mask(topo, src, dsts):
    m = topo.mask(src, dsts[0])
    for d in dsts[1:]:
        m &= topo.mask(src, d)
    return m


def _count(mask):
    return bin(mask).count("1")


def _transfers(topo, src, dsts):
    m = _mask(topo, src, dsts)
    e = [b for b in range(m.bit_length()) if (m >> b) & 1]
    n = len(dsts)
    if n > 1 and len(e) % n == 0 and 128 % (len(e) // n) == 0:
        k = len(e) // n
        return [(sum(1 << b for b in e[i * k:(i + 1) * k]), [dsts[i]]) for i in range(n)]
    return [(m, list(dsts))]


def rank_program(g, core, T, topo):
    rank = T.rank_of(core)
    if rank is None:
        return
    cores = list(T.cores)
    groups, sum_to = _plan(cores, topo)
    gi = rank // GROUP
    members = groups[gi]
    me = rank - members[0]
    add = AluOpType.add
    ring = bool(sum_to[rank])
    assert not ring or len(members) == 3

    def width(sender, dst_ranks, to):
        for mask, ds in _transfers(topo, cores[sender], [cores[d] for d in dst_ranks]):
            if cores[to] in ds:
                return _count(mask)
        assert False

    def send(src, buf, sem, dst_ranks):
        trs, tot = [], 0
        for mask, ds in _transfers(topo, core, [cores[d] for d in dst_ranks]):
            ids = []
            for d in ds:
                assert topo.may_write(core, d)
                rid, pid, _ = topo.addr(d)
                ids.append(DstId(rid=rid, pnc=pid))
            trs.append(RemoteDMATransfer(dst_ids=ids, dma_engine_mask=mask, remote_sem=sem, srcs=[src[:]],
                                         dsts=[buf[:] for _ in ds], alu_op=0))
            tot += _count(mask)
        g.remote_dma_fused(trs, local_sem=T.sem.sent)
        return tot

    if ring:
        g.sync.dma_start(T.ad[:], T.a[:]).then_inc(T.sem.lc, 16)
    g.scalar.dma_start(T.xw[:], T.w[:]).then_inc(T.sem.lw, 16)
    g.scalar.dma_start(T.xa[:], T.a[:]).then_inc(T.sem.la, 16)
    g.tensor.wait_ge(T.sem.la, 16)
    g.tensor.wait_ge(T.sem.lw, 16)
    g.tensor.matmul(T.ps[:], T.xa[:], T.xw[:], True, True).then_inc(T.sem.mm, 1)

    sums = []
    for q in range(gi - 1, -1, -1):
        s = [x for x in groups[q] if rank in sum_to[x]][0]
        sums.append(("sum%d" % q, width(s, sum_to[s], rank)))

    nv = [0]

    def vec(out, in0, name, w):
        g.vector.wait_ge(T.sem[name], w)
        if nv[0]:
            g.vector.wait_ge(T.sem.vs, nv[0])
        g.vector.tensor_tensor(out[:], in0[:], T[name][:], add).then_inc(T.sem.vs, 1)
        nv[0] += 1

    def finish(acc, yterms):
        for name, w in yterms[:-1]:
            vec(acc, acc, name, w)
        name, w = yterms[-1]
        g.vector.wait_ge(T.sem[name], w)
        if nv[0]:
            g.vector.wait_ge(T.sem.vs, nv[0])
        for lo, hi in ((0, H), (H, F)):
            g.vector.tensor_tensor(T.yb[:, lo:hi], acc[:, lo:hi], T[name][:, lo:hi], add).then_inc(T.sem.vs, 1)
            nv[0] += 1

    sent = 0
    halves = False
    if ring:
        d = _turn(cores, topo, members, sum_to)
        nxt, prv = (me + d) % 3, (me - d) % 3
        g.sync.wait_ge(T.sem.ax, width(members[prv], [rank], rank))
        g.sync.dma_start(T.ra[:], T.ar[:]).then_inc(T.sem.lr, 16)
        g.tensor.matmul(T.pg[:], T.xa[:], T.xw[:], True, False)
        g.tensor.wait_ge(T.sem.lr, 16)
        g.tensor.wait_ge(T.sem.xs, width(members[prv], [rank], rank))
        g.tensor.matmul(T.pg[:], T.ra[:], T.rw[:], False, True).then_inc(T.sem.mg, 1)
        g.vector.wait_ge(T.sem.mm, 1)
        g.vector.tensor_copy(T.pb[:], T.ps[:]).then_inc(T.sem.vs, 1)
        nv[0] = 1
        g.vector.wait_ge(T.sem.mg, 1)
        late = ("raw%d" % nxt, width(members[nxt], [rank], rank))
        vec(T.gs, T.pg, late[0], late[1])
        gat = nv[0]
        own_only = prv > me
        acc = T.ps if own_only else T.pg
        yterms = ([late] if nxt < me else []) + sums
        if yterms == [late] and not own_only:
            ysrc, yat = T.gs, gat
        elif not yterms and own_only:
            ysrc, yat = T.pb, 1
        elif not yterms:
            g.vector.wait_ge(T.sem.vs, nv[0])
            g.vector.tensor_copy(T.yb[:], acc[:]).then_inc(T.sem.vs, 1)
            nv[0] += 1
            ysrc, yat = T.yb, nv[0]
        else:
            finish(acc, yterms)
            ysrc, yat, halves = T.yb, nv[0], True
        g.wait_ge(T.sem.lc, 16)
        sent += send(T.ad, T.ar, T.sem.ax, [members[nxt]])
        g.wait_ge(T.sem.lw, 16)
        sent += send(T.xw, T.rw, T.sem.xs, [members[nxt]])
        g.wait_ge(T.sem.vs, 1)
        sent += send(T.pb, T["raw%d" % me], T.sem["raw%d" % me], [members[prv]])
        g.wait_ge(T.sem.vs, gat)
        sent += send(T.gs, T["sum%d" % gi], T.sem["sum%d" % gi], sum_to[rank])
    else:
        after = members[me + 1:]
        g.vector.wait_ge(T.sem.mm, 1)
        if after:
            g.vector.tensor_copy(T.pb[:], T.ps[:]).then_inc(T.sem.vs, 1)
            nv[0] = 1
        yterms = [("raw%d" % k, width(members[k], members[k + 1:], rank)) for k in range(me - 1, -1, -1)] + sums
        assert yterms
        finish(T.ps, yterms)
        ysrc, yat, halves = T.yb, nv[0], True
        if after:
            g.wait_ge(T.sem.vs, 1)
            sent += send(T.pb, T["raw%d" % me], T.sem["raw%d" % me], after)

    if halves:
        g.sync.wait_ge(T.sem.vs, yat - 1)
        g.sync.dma_start(T.y[:, 0:H], ysrc[:, 0:H]).then_inc(T.sem.st, 16)
        g.scalar.wait_ge(T.sem.vs, yat)
        g.scalar.dma_start(T.y[:, H:F], ysrc[:, H:F]).then_inc(T.sem.st, 16)
        g.sync.wait_ge(T.sem.st, 32)
    else:
        g.sync.wait_ge(T.sem.vs, yat)
        g.sync.dma_start(T.y[:], ysrc[:]).then_inc(T.sem.st, 16)
        g.sync.wait_ge(T.sem.st, 16)
    g.wait_ge(T.sem.vs, nv[0])
    if sent:
        g.wait_ge(T.sem.sent, sent)
